import numpy as np
import ml_dtypes


def mxq(x, axis, fmt="e4m3"):
    dtype, down = {"e4m3": (ml_dtypes.float8_e4m3fn, 7), "e5m2": (ml_dtypes.float8_e5m2, 14)}[fmt]
    v = np.moveaxis(np.asarray(x, np.float32).astype(ml_dtypes.bfloat16).astype(np.float64), axis, -1)
    blocks = v.reshape(v.shape[:-1] + (-1, 32))
    amax = np.abs(blocks).max(-1, keepdims=True)
    byte = np.maximum(np.where(amax > 0, np.frexp(amax)[1] - 1 + 127, 0) - down, 1)
    scale = np.exp2(byte - 127.0)
    codes = (blocks / scale).astype(np.float32).astype(dtype).astype(np.float64)
    return np.moveaxis((codes * scale).reshape(v.shape), -1, axis)


WIDE = False


def mx_kscale(k):
    if not WIDE:
        return np.ones(k)
    levels = np.array([10, -10, 5, -5, 0])
    if k % 512:
        return np.exp2(np.random.permutation(np.resize(levels, k // 32))).repeat(32)
    a = np.empty((k // 512, 16))
    for p in range(k // 512):
        a[p, :8] = np.random.permutation(np.resize(levels, 8))
        for g in range(8):
            far = levels[np.abs(levels - a[p, g]) >= 10]
            a[p, g + 8] = far[np.random.randint(len(far))]
    return np.exp2(a.ravel()).repeat(32)


BF16 = ml_dtypes.bfloat16


def bf(x):
    return np.asarray(x, np.float32).astype(BF16)


def f64(x):
    return np.asarray(x).astype(np.float64)


E2M1 = np.array([0.0, 0.5, 1.0, 1.5, 2.0, 3.0, 4.0, 6.0, -0.0, -0.5, -1.0, -1.5, -2.0, -3.0, -4.0, -6.0])


def pack_weight(w, fmt):
    k, n = w.shape
    w = f64(bf(w)).reshape(k // 32, 32, n)
    amax = np.abs(w).max(1)
    if fmt == "e4m3":
        byte = np.frexp(amax)[1] - 1 + 127 - 7
    else:
        mant, ex = np.frexp(amax / 6.0)
        byte = np.where(mant > 0.5, ex, ex - 1) + 127
    byte = np.clip(np.where(amax > 0, byte, 1), 1, 254)
    scaled = (w * np.exp2(127.0 - byte)[:, None, :]).reshape(k, n).astype(np.float32)
    by_word = np.ascontiguousarray(scaled.reshape(k // 512, 128, 4, n).transpose(0, 1, 3, 2))
    if fmt == "e4m3":
        words = by_word.astype(ml_dtypes.float8_e4m3fn).view(np.uint8)
    else:
        c = by_word.astype(ml_dtypes.float4_e2m1fn).view(np.uint8) & 0xF
        words = c[..., 0::2] | (c[..., 1::2] << 4)
    return np.ascontiguousarray(words), np.ascontiguousarray(byte.astype(np.uint8).reshape(k // 512, 16, n))


def unpack_weight(words, scales, fmt):
    g, p, n, _ = words.shape
    if fmt == "e4m3":
        vals = np.ascontiguousarray(words).view(ml_dtypes.float8_e4m3fn).astype(np.float64)
    else:
        nib = np.empty((g, p, n, 4), np.uint8)
        nib[..., 0::2] = words & 0xF
        nib[..., 1::2] = words >> 4
        vals = E2M1[nib]
    vals = vals * np.repeat(np.exp2(scales.astype(np.float64) - 127.0), 8, axis=1)[..., None]
    return vals.transpose(0, 1, 3, 2).reshape(g * 512, n)
def pack4(w):
    words, scales = pack_weight(w, "e2m1")
    return words.reshape(words.shape[0], 128, -1), scales


def unpack4(words, scales):
    return unpack_weight(words.reshape(words.shape[0], 128, -1, 2), scales, "e2m1")


R, S, K, E, F, C = 128, 16, 1024, 512, 1024, 512


def draw0():
    s, v, t = mx_kscale(K), mx_kscale(E), mx_kscale(F)
    wb_words, wb_scales = pack4(np.random.standard_normal((K, F)) / np.sqrt(K) / s[:, None] * t)
    wv_words, wv_scales = pack4(np.random.standard_normal((E, F)) * np.sqrt(2.0 / E) / v[:, None] * t)
    wt_words, wt_scales = pack4(np.random.standard_normal((K, C)) / np.sqrt(K) / s[:, None])
    wo_words, wo_scales = pack_weight(np.random.standard_normal((F, C)) / np.sqrt(F) / t[:, None], "e4m3")
    return {"x": bf(np.random.standard_normal((R * S, K)) * s),
            "phase": bf(np.random.uniform(-3.14, 3.14, (R, E // 2))),
            "band_gain": bf((1.0 + 0.1 * np.random.standard_normal(E)) * v),
            "wb_words": wb_words, "wb_scales": wb_scales,
            "wv_words": wv_words, "wv_scales": wv_scales,
            "hidden_bias": bf(0.3 * np.random.standard_normal(F) * t),
            "wt_words": wt_words, "wt_scales": wt_scales,
            "tint_bias": bf(0.4 * np.random.standard_normal(C)),
            "wo_words": wo_words, "wo_scales": wo_scales,
            "colour_bias": bf(0.4 * np.random.standard_normal(C))}


def sigmoid(z):
    return 1.0 / (1.0 + np.exp(-z))


def softplus(z):
    return np.maximum(z, 0.0) + np.log(1.0 + np.exp(-np.abs(z)))


def core(x, phase, band_gain, wb_words, wb_scales, wv_words, wv_scales, hidden_bias,
              wt_words, wt_scales, tint_bias, wo_words, wo_scales, colour_bias):
    xq = mxq(f64(x), 1, "e4m3")
    a = f64(phase)
    e = np.concatenate([np.sin(a), np.cos(a)], axis=1) * f64(band_gain)
    view = mxq(e, 1, "e4m3") @ unpack4(wv_words, wv_scales)
    bottleneck = xq @ unpack4(wb_words, wb_scales)
    h = np.maximum(bottleneck.reshape(R, S, F) + view[:, None, :] + f64(hidden_bias), 0.0).reshape(R * S, F)
    tint = sigmoid((xq @ unpack4(wt_words, wt_scales)) + f64(tint_bias))
    z = (mxq(h, 1, "e4m3") @ unpack_weight(wo_words, wo_scales, "e4m3")) + f64(colour_bias)
    return tint * softplus(z)


def e4m3fn_bytes(y):
    return np.clip(np.asarray(y, np.float64), -448.0, 448.0).astype(np.float32).astype(ml_dtypes.float8_e4m3fn).view(np.uint8)


def e4m3fn_values(b):
    return np.asarray(b, np.uint8).view(ml_dtypes.float8_e4m3fn).astype(np.float64)


def setup_inputs():
    d = draw0()
    x0 = np.asarray(d['x']).astype(np.float64)
    s = (np.max(np.abs(x0), axis=(0,), keepdims=True) / 448.0).astype(np.float32)
    out = {}
    for k, v in d.items():
        if k == 'x':
            out['x_bytes'] = e4m3fn_bytes(x0 / s.astype(np.float64))
            out['x_scale'] = s
        else:
            out[k] = v
    return out


def reference(x_bytes, x_scale, phase, band_gain, wb_words, wb_scales, wv_words, wv_scales, hidden_bias, wt_words, wt_scales, tint_bias, wo_words, wo_scales, colour_bias):
    return core(e4m3fn_values(x_bytes) * x_scale.astype(np.float64), phase, band_gain, wb_words, wb_scales, wv_words, wv_scales, hidden_bias, wt_words, wt_scales, tint_bias, wo_words, wo_scales, colour_bias)

@@ -1,0 +1,468 @@
+import math
+from contextlib import ExitStack
+
+import concourse.mybir as mybir
+from concourse.masks import make_identity
+
+R, S, K, E, F, C = 128, 16, 1024, 512, 1024, 512
+FLOPS = 2 * (R * E * F + R * S * K * (F + C) + R * S * F * C)
+
+F32 = mybir.dt.float32
+BF16 = mybir.dt.bfloat16
+I32 = mybir.dt.int32
+U32 = mybir.dt.uint32
+U8 = mybir.dt.uint8
+FP8 = mybir.dt.float8_e4m3fn
+FP8X4 = mybir.dt.float8_e4m3fn_x4
+FP4X4 = mybir.dt.float4_e2m1fn_x4
+ALU = mybir.AluOpType
+ACT = mybir.ActivationFunctionType
+
+P = 128
+G = 2
+NJ = 4
+NM = S // NJ
+W = NJ * P
+NC = C // P
+TINY = 2.0**-64
+
+
+def tile_nerf_view_colour_head_f7_kernel(
+    tc, x_bytes, x_scale, phase, band_gain, wb_words, wb_scales, wv_words, wv_scales, hidden_bias,
+    wt_words, wt_scales, tint_bias, wo_words, wo_scales, colour_bias, out,
+):
+    nc = tc.nc
+    with ExitStack() as ctx:
+        keep = ctx.enter_context(tc.tile_pool(name="keep", bufs=1))
+        work = ctx.enter_context(tc.tile_pool(name="work", bufs=2))
+        psum = ctx.enter_context(tc.psum_pool(name="psum", bufs=2))
+        ctx.enter_context(tc.manual_schedule())
+
+        def kt(name, shape, dtype):
+            return keep.tile(shape, dtype, name=name, align_bytes=64)
+
+        def wt_(name, shape, dtype, bufs=2):
+            return work.tile(shape, dtype, name=name, align_bytes=64, bufs=bufs)
+
+        def bank(tag, bufs):
+            return psum.tile([P, 512], F32, name=tag, bufs=bufs)
+
+        ident = kt("ident", [P, P], F32)
+        identb = kt("identb", [P, P], BF16)
+        xs = kt("xs", [P, K], F32)
+        xraw = [kt(f"xraw{m}", [P, NJ * K], U8) for m in range(NM)]
+        ph = kt("ph", [P, E // 2], BF16)
+        gain = kt("gain", [P, E], BF16)
+        hb = kt("hb", [P, G, 4], BF16)
+        brow = kt("brow", [P, P], BF16)
+        bcol = kt("bcol", [P, 2 * NC], F32)
+        wb = kt("wb", [P, G, 2 * F], U8)
+        wbs = kt("wbs", [P, G, F], U8)
+        wbp = kt("wbp", [P, G, 2 * F], U8)
+        wbsp = kt("wbsp", [P, G, F], U8)
+        wv = kt("wv", [P, 2 * F], U8)
+        wvs = kt("wvs", [P, F], U8)
+        wt = kt("wt", [P, G, 2 * C], U8)
+        wts = kt("wts", [P, G, C], U8)
+        wo = kt("wo", [P, G, 4 * C], U8)
+        wos = kt("wos", [P, G, C], U8)
+        vb = kt("vb", [P, G, P, 4], F32)
+
+        xv = x_bytes.rearrange("(r s) k -> r (s k)", s=S)
+        ov = out.rearrange("(r s) c -> r s c", s=S)
+
+        def load_scales(tile_, dram):
+            for q in range(4):
+                nc.sync.dma_start(
+                    out=tile_[32 * q : 32 * q + 4].bitcast(I32),
+                    in_=dram[:, 4 * q : 4 * q + 4, :].rearrange("g q n -> q g n").bitcast(I32),
+                )
+
+        warm = kt("warm", [P, 1], F32)
+        nc.vector.memset(warm[:], 0.0)
+        nc.scalar.activation(out=warm[:], in_=warm[:], func=ACT.Sin)
+        nc.vector.memset(wvs[:].bitcast(I32), 0)
+        nc.vector.memset(brow[:], 0.0)
+        for t_ in (wbs, wts, wos):
+            nc.vector.memset(t_[:].rearrange("p g n -> p (g n)").bitcast(I32), 0)
+        make_identity(nc, ident[:])
+        nc.gpsimd.tensor_copy(out=identb[:], in_=ident[:])
+
+        def load_x(m, j0, j1):
+            nc.sync.dma_start(out=xraw[m][:, j0 * K : j1 * K], in_=xv[:, (m * NJ + j0) * K : (m * NJ + j1) * K])
+
+        nc.sync.dma_start(out=ph[:], in_=phase)
+        nc.sync.dma_start(out=xs[:], in_=x_scale.rearrange("o k -> (o k)").partition_broadcast(P))
+        load_x(0, 0, 1)
+        load_x(0, 1, 2)
+        nc.sync.dma_start(out=gain[:], in_=band_gain.partition_broadcast(P))
+        load_x(0, 2, 4)
+        nc.sync.dma_start(out=wv[:].bitcast(I32), in_=wv_words[0].bitcast(I32))
+        for q in range(4):
+            nc.sync.dma_start(out=wvs[32 * q : 32 * q + 4].bitcast(I32), in_=wv_scales[0, 4 * q : 4 * q + 4, :].bitcast(I32))
+        load_scales(wbs, wb_scales)
+        nc.sync.dma_start(out=wb[:].bitcast(I32), in_=wb_words.rearrange("g p n -> p g n").bitcast(I32))
+        nc.sync.dma_start(out=hb[:], in_=hidden_bias.rearrange("(g p t) -> p g t", g=G, t=4))
+        nc.sync.dma_start(out=brow[0:NC, :], in_=tint_bias.rearrange("(a p) -> a p", p=P))
+        nc.sync.dma_start(out=brow[NC : 2 * NC, :], in_=colour_bias.rearrange("(a p) -> a p", p=P))
+        load_x(1, 0, 4)
+        load_scales(wts, wt_scales)
+        nc.sync.dma_start(out=wt[:].bitcast(I32), in_=wt_words.rearrange("g p n -> p g n").bitcast(I32))
+        load_scales(wos, wo_scales)
+        nc.sync.dma_start(
+            out=wo[:].bitcast(I32), in_=wo_words.rearrange("g p n t -> p g (n t)").bitcast(I32)
+        )
+        for m in range(2, NM):
+            load_x(m, 0, 4)
+
+        xg, xc, xsc = {}, {}, {}
+
+        def widen(m, j):
+            if j == 0:
+                xg[m] = wt_("xg", [P, G, NJ, P, 4], BF16)
+                xc[m] = wt_("xc", [P, G, W], U32, bufs=3)
+                xsc[m] = wt_("xsc", [P, G, W], U8, bufs=3)
+            xb = wt_("xb", [P, K], BF16, bufs=4)
+            nc.vector.tensor_tensor(
+                out=xb[:], in0=xraw[m][:, j * K : (j + 1) * K].bitcast(FP8), in1=xs[:], op=ALU.mult
+            )
+            return xb
+
+        def turn(m, j, xb):
+            xw = xb[:].bitcast(F32)
+            tp = bank("tp", 2)
+            for g in range(G):
+                for u in range(2):
+                    nc.tensor.transpose(
+                        tp[:, (2 * g + u) * P : (2 * g + u + 1) * P],
+                        xw[:, 256 * g + u : 256 * (g + 1) : 2],
+                        ident[:],
+                    )
+            return tp
+
+        def words(m, j, tp):
+            nc.scalar.copy(
+                out=xg[m][:, :, j].rearrange("p g r t -> p g (r t)").bitcast(F32).rearrange("p g (r u) -> p g r u", u=2),
+                in_=tp[:].rearrange("p (g u r) -> p g r u", g=G, u=2),
+            )
+
+        def quant_x(m, g):
+            nc.vector.quantize_mx(
+                out=xc[m][:, g].bitcast(FP8X4), scales=xsc[m][:, g],
+                in_=xg[m][:, g].rearrange("p j r t -> p (j r t)"),
+            )
+
+        hp, hc, hsc = {}, {}, {}
+
+        def bottleneck(m, h, j):
+            acc = bank("acc", 2)
+            cols = slice(j * P, (j + 1) * P)
+            for t in range(4):
+                n0 = (h * 4 + t) * P
+                for g in range(G):
+                    nc.tensor.matmul_mx(
+                        out=acc[:, t * P : (t + 1) * P],
+                        lhsT=wbp[:, g, 2 * n0 : 2 * (n0 + P)].bitcast(FP4X4),
+                        lhsT_scale=wbsp[:, g, n0 : n0 + P],
+                        rhs=xc[m][:, g, cols].bitcast(FP8X4),
+                        rhs_scale=xsc[m][:, g, cols],
+                        start=(g == 0),
+                        stop=(g == G - 1),
+                    )
+            return acc
+
+        def add_view(m, h, j, acc):
+            if j == 0:
+                hp[m, h] = wt_("hp", [P, NJ, P, 4], BF16, bufs=4)
+                if h == 0:
+                    hc[m] = wt_("hc", [P, G, W], U32)
+                    hsc[m] = wt_("hsc", [P, G, W], U8)
+            nc.vector.tensor_tensor(
+                out=hp[m, h][:, j], in0=acc[:].rearrange("p (t r) -> p r t", t=4), in1=vb[:, h], op=ALU.add
+            )
+
+        def relu(m, h, j0, j1):
+            v = hp[m, h][:, j0:j1].rearrange("p j r t -> p (j r t)")
+            nc.vector.tensor_scalar_max(v, v, 0.0)
+
+        def quant_h(m, h, j0, j1):
+            cols = slice(j0 * P, j1 * P)
+            nc.vector.quantize_mx(
+                out=hc[m][:, h, cols].bitcast(FP8X4), scales=hsc[m][:, h, cols],
+                in_=hp[m, h][:, j0:j1].rearrange("p j r t -> p (j r t)"),
+            )
+
+        st, sz, zt, pr = {}, {}, {}, {}
+
+        def tint(m, c):
+            if c == 0:
+                st[m] = wt_("st", [P, NC, W], F32)
+            acc = bank("zt", 4)
+            for g in range(G):
+                nc.tensor.matmul_mx(
+                    out=acc[:],
+                    lhsT=wt[:, g, 2 * c * P : 2 * (c + 1) * P].bitcast(FP4X4),
+                    lhsT_scale=wts[:, g, c * P : (c + 1) * P],
+                    rhs=xc[m][:, g].bitcast(FP8X4),
+                    rhs_scale=xsc[m][:, g],
+                    start=(g == 0),
+                    stop=(g == G - 1),
+                )
+            nc.scalar.activation(out=st[m][:, c], in_=acc[:], func=ACT.Sigmoid, bias=bcol[:, c : c + 1])
+
+        def radiance(m, c, j0, j1):
+            if c == 0 and j0 == 0:
+                sz[m] = wt_("sz", [P, NC, W], F32)
+            if j0 == 0:
+                zt[m, c] = bank("zt", 4)
+            acc = zt[m, c]
+            cols = slice(j0 * P, j1 * P)
+            for h in range(G):
+                nc.tensor.matmul_mx(
+                    out=acc[:, cols],
+                    lhsT=wo[:, h, 4 * c * P : 4 * (c + 1) * P].bitcast(FP8X4),
+                    lhsT_scale=wos[:, h, c * P : (c + 1) * P],
+                    rhs=hc[m][:, h, cols].bitcast(FP8X4),
+                    rhs_scale=hsc[m][:, h, cols],
+                    start=(h == 0),
+                    stop=(h == G - 1),
+                )
+            nc.scalar.activation(
+                out=sz[m][:, c, cols], in_=acc[:, cols], func=ACT.Sigmoid, bias=bcol[:, NC + c : NC + c + 1]
+            )
+
+        def log(m, c, j0=0, j1=NJ):
+            v = sz[m][:, c, j0 * P : j1 * P]
+            nc.scalar.activation(out=v, in_=v, func=ACT.Ln, bias=TINY)
+
+        def softplus(m, c, j0=0, j1=NJ):
+            if c == 0 and j0 == 0:
+                pr[m] = wt_("pr", [P, NC, W], F32)
+            cols = slice(j0 * P, j1 * P)
+            nc.vector.scalar_tensor_tensor(
+                out=pr[m][:, c, cols], in0=zt[m, c][:, cols], scalar=bcol[:, NC + c : NC + c + 1],
+                in1=sz[m][:, c, cols], op0=ALU.add, op1=ALU.subtract,
+            )
+
+        def product(eng, m, c, j0=0, j1=NJ):
+            v = pr[m][:, c, j0 * P : j1 * P]
+            eng.tensor_tensor(out=v, in0=v, in1=st[m][:, c, j0 * P : j1 * P], op=ALU.mult)
+
+        def emit(m, j, on_vector=False):
+            tp = bank("tp", 2)
+            for c in range(NC):
+                nc.tensor.transpose(tp[:, c * P : (c + 1) * P], pr[m][:, c, j * P : (j + 1) * P], ident[:])
+            ot = wt_("ot", [P, C], F32, bufs=4)
+            if on_vector:
+                nc.vector.tensor_scalar_max(ot[:], tp[:], 0.0)
+            else:
+                nc.scalar.activation(out=ot[:], in_=tp[:], func=ACT.Relu)
+            nc.sync.dma_start(out=ov[:, NJ * m + j, :], in_=ot[:])
+
+        em = kt("em", [P, E], F32)
+        eb = kt("eb", [P, E], BF16)
+        eg = kt("eg", [P, P, 4], BF16)
+        ec = kt("ec", [P, P], U32)
+        esc = kt("esc", [P, P], U8)
+        vw = kt("vw", [P, G, 4, P], F32)
+        hE = E // 2
+
+        nc.scalar.activation(out=em[:, 0:hE], in_=ph[:], func=ACT.Sin)
+        nc.scalar.activation(out=em[:, hE:E], in_=ph[:], func=ACT.Abs)
+        nc.scalar.activation(out=em[:, hE:E], in_=em[:, hE:E], func=ACT.Sin, bias=math.pi / 2, scale=-1.0)
+
+        def permute_scales(g):
+            nc.vector.tensor_copy(
+                out=wbsp[:, g].rearrange("p (h t m) -> p h t m", h=G, t=4),
+                in_=wbs[:, g].rearrange("p (h m t) -> p h t m", h=G, t=4),
+            )
+
+        def permute(g, h):
+            nc.vector.tensor_copy(
+                out=wbp[:, g, 1024 * h : 1024 * (h + 1)].rearrange("p (t m b) -> p t m b", t=4, b=2),
+                in_=wb[:, g, 1024 * h : 1024 * (h + 1)].rearrange("p (m t b) -> p t m b", t=4, b=2),
+            )
+
+        def view_product(h):
+            acc = bank("acc", 2)
+            nc.tensor.matmul_mx(
+                out=acc[:], lhsT=ec[:].bitcast(FP8X4), lhsT_scale=esc[:],
+                rhs=wv[:, 1024 * h : 1024 * (h + 1)].bitcast(FP4X4), rhs_scale=wvs[:, 512 * h : 512 * (h + 1)],
+                start=True, stop=True,
+            )
+            return acc
+
+        def view_out(h, acc):
+            nc.scalar.copy(out=vw[:, h], in_=acc[:].rearrange("p (m t) -> p t m", t=4))
+
+        def view_turn(h):
+            tp = bank("tp", 2)
+            for t in range(4):
+                nc.tensor.transpose(tp[:, t * P : (t + 1) * P], vw[:, h, t], ident[:])
+            return tp
+
+        def view_bias(h, tp):
+            nc.vector.tensor_tensor(
+                out=vb[:, h], in0=tp[:].rearrange("p (t r) -> p r t", t=4),
+                in1=hb[:, h].unsqueeze(1).to_broadcast([P, P, 4]), op=ALU.add,
+            )
+
+        xbs, tps, accs = {}, {}, {}
+
+        def wide(m, j):
+            if m < NM:
+                xbs[m, j] = widen(m, j)
+
+        def tr(m, j):
+            if m < NM:
+                tps[m, j] = turn(m, j, xbs[m, j])
+
+        def wr(m, j):
+            if m < NM:
+                words(m, j, tps[m, j])
+
+        def qx(m, g):
+            if m < NM:
+                quant_x(m, g)
+
+        def mul(m, h, j):
+            if m < NM:
+                accs[m, h, j] = bottleneck(m, h, j)
+
+        def add(m, h, j):
+            add_view(m, h, j, accs[m, h, j])
+
+        def tn(m, c):
+            if m < NM:
+                tint(m, c)
+
+        def soft(m, c):
+            if m >= 0:
+                log(m, c)
+                softplus(m, c)
+
+        def prod(m, c):
+            if m >= 0:
+                product(nc.gpsimd, m, c)
+
+        def em_(m, j):
+            if m >= 0:
+                emit(m, j)
+
+        def finish(m, j0, j1):
+            relu(m, 0, j0, j1)
+            relu(m, 1, j0, j1)
+            quant_h(m, 0, j0, j1)
+            quant_h(m, 1, j0, j1)
+            for c in range(NC):
+                radiance(m, c, j0, j1)
+
+        wide(0, 0)
+        tr(0, 0)
+        nc.vector.tensor_tensor(out=eb[:], in0=em[:], in1=gain[:], op=ALU.mult)
+        tp = bank("tp", 2)
+        ew = eb[:].bitcast(F32)
+        for u in range(2):
+            nc.tensor.transpose(tp[:, u * P : (u + 1) * P], ew[:, u:256:2], ident[:])
+        nc.scalar.copy(
+            out=eg[:].rearrange("p r t -> p (r t)").bitcast(F32).rearrange("p (r u) -> p r u", u=2),
+            in_=tp[:, 0:256].rearrange("p (u r) -> p r u", u=2),
+        )
+        wide(0, 1)
+        wr(0, 0)
+        tr(0, 1)
+        wide(0, 2)
+        tr(0, 2)
+        wide(0, 3)
+        wr(0, 1)
+        tr(0, 3)
+        permute_scales(0)
+        nc.vector.quantize_mx(out=ec[:].bitcast(FP8X4), scales=esc[:], in_=eg[:].rearrange("p r t -> p (r t)"))
+        permute(0, 0)
+        va0 = view_product(0)
+        permute(1, 0)
+        va1 = view_product(1)
+        wr(0, 2)
+        wr(0, 3)
+        qx(0, 0)
+        view_out(0, va0)
+        vt0 = view_turn(0)
+        view_out(1, va1)
+        vt1 = view_turn(1)
+        qx(0, 1)
+        view_bias(0, vt0)
+        bp = psum.tile([P, P], BF16, name="bp", tag="tp", bufs=2)
+        nc.tensor.transpose(bp[:], brow[:], identb[:])
+        nc.scalar.copy(out=bcol[:], in_=bp[:, 0 : 2 * NC])
+        tn(0, 0)
+        tn(0, 1)
+        permute_scales(1)
+        mul(0, 0, 0)
+        tn(0, 2)
+        permute(0, 1)
+        permute(1, 1)
+        mul(0, 1, 0)
+        view_bias(1, vt1)
+
+        for m in range(NM):
+            n, p, q = m + 1, m - 1, m - 2
+            wide(n, 0)
+            tr(n, 0)
+            wide(n, 1)
+            tr(n, 1)
+            add(m, 0, 0)
+            mul(m, 0, 1)
+            add(m, 1, 0)
+            mul(m, 0, 2)
+            wide(n, 2)
+            wr(n, 0)
+            tr(n, 2)
+            add(m, 0, 1)
+            mul(m, 1, 1)
+            wide(n, 3)
+            wr(n, 1)
+            tr(n, 3)
+            add(m, 0, 2)
+            mul(m, 0, 3)
+            add(m, 1, 1)
+            mul(m, 1, 2)
+            soft(p, 0)
+            soft(p, 1)
+            wr(n, 2)
+            wr(n, 3)
+            qx(n, 0)
+            prod(p, 0)
+            soft(p, 2)
+            soft(p, 3)
+            em_(q, 0)
+            prod(p, 1)
+            em_(q, 1)
+            tn(m, 3)
+            prod(p, 2)
+            prod(p, 3)
+            add(m, 0, 3)
+            mul(m, 1, 3)
+            qx(n, 1)
+            tn(n, 0)
+            tn(n, 1)
+            if n == NM:
+                finish(m, 0, 2)
+            add(m, 1, 2)
+            mul(n, 0, 0)
+            tn(n, 2)
+            add(m, 1, 3)
+            mul(n, 1, 0)
+            em_(q, 2)
+            em_(q, 3)
+            finish(m, 0 if n < NM else 2, NJ)
+        m = NM - 1
+        for j in range(NJ):
+            emit(m - 1, j, on_vector=True)
+        for j in (0, 2):
+            for c in range(NC):
+                log(m, c, j, j + 2)
+                softplus(m, c, j, j + 2)
+            for c in range(NC):
+                product(nc.vector, m, c, j, j + 2)
+            emit(m, j)
+            emit(m, j + 1, on_vector=True)

@@ -25,6 +25,15 @@ NM = S // NJ
 W = NJ * P
 NC = C // P
 TINY = 2.0**-64
+PARTS = [(0, 2), (2, 4)]
+ON_VECTOR = {(3, 1), (3, 3), (2, 0), (2, 1)}
+ORDER = """
+L- O-- O-- VM+ VT+ R0- L- SA E-- VT+ E-- SA D- XU+ E-- E-- B0+ SA+ B0+ SA+ R1 SIN+ SZ A1- Z-- Z D- QH1- A1--
+SZ SZ W++ EB++ SZ VC W TN- T++ T++ C+ B0+ C TN+ T++ PW+ VC-- SZ QX B0+ B1+ XW-- Z- XW- L- P-- SZ QH0 T++ SZ SZ
+BC++ Z- QH1- R1 BT-- B1+ VB+ VM++ P-- L D- PS++ C++ TN+ PW++ D- B1+ P-- R0+ P-- O- A0-- XU+ ET++ P- QH0 Z- L
+L-- A0-- O- XC+ D- TN+ PS++ XT-- W Z- PW+ A1 W-- C+ A1+ L-- D- P- EQ+ PW++ B1+ A0-- P- Z D- QX++ A0+ VB D- P-
+Z L
+"""
 
 
 def tile_nerf_view_colour_head_f7_kernel(
@@ -52,8 +61,10 @@ def tile_nerf_view_colour_head_f7_kernel(
         xs = kt("xs", [P, K], F32)
         xraw = [kt(f"xraw{m}", [P, NJ * K], U8) for m in range(NM)]
         ph = kt("ph", [P, E // 2], BF16)
-        gain = kt("gain", [P, E], BF16)
+        gain = kt("gain", [P, 4], BF16)
         hb = kt("hb", [P, G, 4], BF16)
+        srow = kt("srow", [P, P], F32)
+        scol = kt("scol", [P, K // P], F32)
         brow = kt("brow", [P, P], BF16)
         bcol = kt("bcol", [P, 2 * NC], F32)
         wb = kt("wb", [P, G, 2 * F], U8)
@@ -78,36 +89,37 @@ def tile_nerf_view_colour_head_f7_kernel(
                     in_=dram[:, 4 * q : 4 * q + 4, :].rearrange("g q n -> q g n").bitcast(I32),
                 )
 
-        warm = kt("warm", [P, 1], F32)
-        nc.vector.memset(warm[:], 0.0)
-        nc.scalar.activation(out=warm[:], in_=warm[:], func=ACT.Sin)
-        nc.vector.memset(wvs[:].bitcast(I32), 0)
-        nc.vector.memset(brow[:], 0.0)
-        for t_ in (wbs, wts, wos):
-            nc.vector.memset(t_[:].rearrange("p g n -> p (g n)").bitcast(I32), 0)
-        make_identity(nc, ident[:])
-        nc.gpsimd.tensor_copy(out=identb[:], in_=ident[:])
-
         def load_x(m, j0, j1):
             nc.sync.dma_start(out=xraw[m][:, j0 * K : j1 * K], in_=xv[:, (m * NJ + j0) * K : (m * NJ + j1) * K])
 
+        warm = kt("warm", [P, 1], F32)
+        nc.vector.memset(srow[:], 0.0)
+        nc.vector.memset(warm[:], 0.0)
+        nc.scalar.activation(out=warm[:], in_=warm[:], func=ACT.Sin)
+        make_identity(nc, ident[:])
+        nc.vector.memset(wbs[:].rearrange("p g n -> p (g n)").bitcast(I32), 0)
+        nc.vector.memset(wvs[:].bitcast(I32), 0)
+        nc.vector.memset(brow[:], 0.0)
+        for t_ in (wts, wos):
+            nc.vector.memset(t_[:].rearrange("p g n -> p (g n)").bitcast(I32), 0)
+        nc.gpsimd.tensor_copy(out=identb[:], in_=ident[:])
+
+        nc.sync.dma_start(out=srow[0 : K // P, :], in_=x_scale.rearrange("o (a p) -> (o a) p", p=P))
         nc.sync.dma_start(out=ph[:], in_=phase)
-        nc.sync.dma_start(out=xs[:], in_=x_scale.rearrange("o k -> (o k)").partition_broadcast(P))
-        load_x(0, 0, 1)
-        load_x(0, 1, 2)
-        nc.sync.dma_start(out=gain[:], in_=band_gain.partition_broadcast(P))
+        load_x(0, 0, 2)
         load_x(0, 2, 4)
+        nc.sync.dma_start(out=gain[:], in_=band_gain.rearrange("(p t) -> p t", t=4))
+        nc.sync.dma_start(out=wb[:].bitcast(I32), in_=wb_words.rearrange("g p n -> p g n").bitcast(I32))
         nc.sync.dma_start(out=wv[:].bitcast(I32), in_=wv_words[0].bitcast(I32))
+        load_scales(wbs, wb_scales)
         for q in range(4):
             nc.sync.dma_start(out=wvs[32 * q : 32 * q + 4].bitcast(I32), in_=wv_scales[0, 4 * q : 4 * q + 4, :].bitcast(I32))
-        load_scales(wbs, wb_scales)
-        nc.sync.dma_start(out=wb[:].bitcast(I32), in_=wb_words.rearrange("g p n -> p g n").bitcast(I32))
         nc.sync.dma_start(out=hb[:], in_=hidden_bias.rearrange("(g p t) -> p g t", g=G, t=4))
         nc.sync.dma_start(out=brow[0:NC, :], in_=tint_bias.rearrange("(a p) -> a p", p=P))
         nc.sync.dma_start(out=brow[NC : 2 * NC, :], in_=colour_bias.rearrange("(a p) -> a p", p=P))
-        load_x(1, 0, 4)
         load_scales(wts, wt_scales)
         nc.sync.dma_start(out=wt[:].bitcast(I32), in_=wt_words.rearrange("g p n -> p g n").bitcast(I32))
+        load_x(1, 0, 4)
         load_scales(wos, wo_scales)
         nc.sync.dma_start(
             out=wo[:].bitcast(I32), in_=wo_words.rearrange("g p n t -> p g (n t)").bitcast(I32)
@@ -115,47 +127,136 @@ def tile_nerf_view_colour_head_f7_kernel(
         for m in range(2, NM):
             load_x(m, 0, 4)
 
-        xg, xc, xsc = {}, {}, {}
+        em = kt("em", [P, 4, P], F32)
+        eg = kt("eg", [P, P, 4], BF16)
+        ec = kt("ec", [P, P], U32)
+        esc = kt("esc", [P, P], U8)
+        vw = kt("vw", [P, G, 4, P], F32)
+        half = P // 2
+        bk = {}
+        xb, xg, xc, xsc, hp, hc, hsc, st, sz, pr = {}, {}, {}, {}, {}, {}, {}, {}, {}, {}
+
+        def turn_scales():
+            bk["XT"] = bank("tp", 2)
+            nc.tensor.transpose(bk["XT"][:, 0:P], srow[:], ident[:])
+
+        def scale_columns():
+            nc.scalar.copy(out=scol[:], in_=bk["XT"][:, 0 : K // P])
+
+        def spread_scales(v):
+            bk["XU", v] = bank("tp", 2)
+            for a in range(4):
+                nc.tensor.transpose(
+                    bk["XU", v][:, a * P : (a + 1) * P], scol[:, 4 * v + a : 4 * v + a + 1].to_broadcast([P, P]), ident[:]
+                )
+
+        def scales_out(v):
+            cols = slice(512 * v, 512 * (v + 1))
+            if v == 0:
+                nc.scalar.copy(out=xs[:, cols], in_=bk["XU", v][:])
+            else:
+                nc.vector.tensor_copy(out=xs[:, cols], in_=bk["XU", v][:])
+
+        def sines():
+            angle = ph[:].rearrange("r (p t) -> r t p", t=4)
+            nc.scalar.activation(out=em[:, :, 0:half], in_=angle, func=ACT.Sin)
+            nc.scalar.activation(out=em[:, :, half:P], in_=angle, func=ACT.Abs)
+            nc.scalar.activation(
+                out=em[:, :, half:P], in_=em[:, :, half:P], func=ACT.Sin, bias=math.pi / 2, scale=-1.0
+            )
+
+        def turn_embed():
+            bk["E"] = bank("tp", 2)
+            for t in range(4):
+                nc.tensor.transpose(bk["E"][:, t * P : (t + 1) * P], em[:, t], ident[:])
+
+        def embed():
+            nc.vector.tensor_tensor(
+                out=eg[:], in0=bk["E"][:].rearrange("p (t r) -> p r t", t=4),
+                in1=gain[:].unsqueeze(1).to_broadcast([P, P, 4]), op=ALU.mult,
+            )
+
+        def quant_embed():
+            nc.vector.quantize_mx(out=ec[:].bitcast(FP8X4), scales=esc[:], in_=eg[:].rearrange("p r t -> p (r t)"))
+
+        def view_product(h):
+            bk["VM", h] = bank("acc", 2)
+            nc.tensor.matmul_mx(
+                out=bk["VM", h][:], lhsT=ec[:].bitcast(FP8X4), lhsT_scale=esc[:],
+                rhs=wv[:, 1024 * h : 1024 * (h + 1)].bitcast(FP4X4), rhs_scale=wvs[:, 512 * h : 512 * (h + 1)],
+                start=True, stop=True,
+            )
+
+        def view_out(h):
+            nc.scalar.copy(out=vw[:, h], in_=bk["VM", h][:].rearrange("p (m t) -> p t m", t=4))
+
+        def view_turn(h):
+            bk["VT", h] = bank("tp", 2)
+            for t in range(4):
+                nc.tensor.transpose(bk["VT", h][:, t * P : (t + 1) * P], vw[:, h, t], ident[:])
+
+        def view_done(h):
+            nc.vector.tensor_tensor(
+                out=vb[:, h], in0=bk["VT", h][:].rearrange("p (t r) -> p r t", t=4),
+                in1=hb[:, h].unsqueeze(1).to_broadcast([P, P, 4]), op=ALU.add,
+            )
+
+        def permute_scales(g):
+            nc.vector.tensor_copy(
+                out=wbsp[:, g].rearrange("p (h t m) -> p h t m", h=G, t=4),
+                in_=wbs[:, g].rearrange("p (h m t) -> p h t m", h=G, t=4),
+            )
+
+        def permute(i):
+            h, g = divmod(i, G)
+            cols = slice(1024 * h, 1024 * (h + 1))
+            nc.vector.tensor_copy(
+                out=wbp[:, g, cols].rearrange("p (t m b) -> p t m b", t=4, b=2),
+                in_=wb[:, g, cols].rearrange("p (m t b) -> p t m b", t=4, b=2),
+            )
+
+        def turn_bias():
+            bk["BT"] = psum.tile([P, P], BF16, name="bp", tag="tp", bufs=2)
+            nc.tensor.transpose(bk["BT"][:], brow[:], identb[:])
+
+        def bias_columns():
+            nc.scalar.copy(out=bcol[:], in_=bk["BT"][:, 0 : 2 * NC])
 
         def widen(m, j):
-            if j == 0:
-                xg[m] = wt_("xg", [P, G, NJ, P, 4], BF16)
-                xc[m] = wt_("xc", [P, G, W], U32, bufs=3)
-                xsc[m] = wt_("xsc", [P, G, W], U8, bufs=3)
-            xb = wt_("xb", [P, K], BF16, bufs=4)
+            xb[m, j] = wt_("xb", [P, K], BF16, bufs=6)
             nc.vector.tensor_tensor(
-                out=xb[:], in0=xraw[m][:, j * K : (j + 1) * K].bitcast(FP8), in1=xs[:], op=ALU.mult
+                out=xb[m, j][:], in0=xraw[m][:, j * K : (j + 1) * K].bitcast(FP8), in1=xs[:], op=ALU.mult
             )
-            return xb
 
-        def turn(m, j, xb):
-            xw = xb[:].bitcast(F32)
-            tp = bank("tp", 2)
+        def turn(m, j):
+            xw = xb[m, j][:].bitcast(F32)
+            bk["T", m, j] = bank("tp", 2)
             for g in range(G):
                 for u in range(2):
                     nc.tensor.transpose(
-                        tp[:, (2 * g + u) * P : (2 * g + u + 1) * P],
-                        xw[:, 256 * g + u : 256 * (g + 1) : 2],
-                        ident[:],
+                        bk["T", m, j][:, (2 * g + u) * P : (2 * g + u + 1) * P],
+                        xw[:, 256 * g + u : 256 * (g + 1) : 2], ident[:],
                     )
-            return tp
 
-        def words(m, j, tp):
+        def words(m, j):
+            if m not in xg:
+                xg[m] = wt_("xg", [P, G, NJ, P, 4], BF16, bufs=3)
             nc.scalar.copy(
                 out=xg[m][:, :, j].rearrange("p g r t -> p g (r t)").bitcast(F32).rearrange("p g (r u) -> p g r u", u=2),
-                in_=tp[:].rearrange("p (g u r) -> p g r u", g=G, u=2),
+                in_=bk["T", m, j][:].rearrange("p (g u r) -> p g r u", g=G, u=2),
             )
 
         def quant_x(m, g):
+            if m not in xc:
+                xc[m] = wt_("xc", [P, G, W], U32, bufs=3)
+                xsc[m] = wt_("xsc", [P, G, W], U8, bufs=3)
             nc.vector.quantize_mx(
                 out=xc[m][:, g].bitcast(FP8X4), scales=xsc[m][:, g],
                 in_=xg[m][:, g].rearrange("p j r t -> p (j r t)"),
             )
 
-        hp, hc, hsc = {}, {}, {}
-
         def bottleneck(m, h, j):
-            acc = bank("acc", 2)
+            acc = bk["B", m, h, j] = bank("acc", 2)
             cols = slice(j * P, (j + 1) * P)
             for t in range(4):
                 n0 = (h * 4 + t) * P
@@ -169,16 +270,12 @@ def tile_nerf_view_colour_head_f7_kernel(
                         start=(g == 0),
                         stop=(g == G - 1),
                     )
-            return acc
 
-        def add_view(m, h, j, acc):
-            if j == 0:
+        def add_view(m, h, j):
+            if (m, h) not in hp:
                 hp[m, h] = wt_("hp", [P, NJ, P, 4], BF16, bufs=4)
-                if h == 0:
-                    hc[m] = wt_("hc", [P, G, W], U32)
-                    hsc[m] = wt_("hsc", [P, G, W], U8)
             nc.vector.tensor_tensor(
-                out=hp[m, h][:, j], in0=acc[:].rearrange("p (t r) -> p r t", t=4), in1=vb[:, h], op=ALU.add
+                out=hp[m, h][:, j], in0=bk["B", m, h, j][:].rearrange("p (t r) -> p r t", t=4), in1=vb[:, h], op=ALU.add
             )
 
         def relu(m, h, j0, j1):
@@ -186,21 +283,20 @@ def tile_nerf_view_colour_head_f7_kernel(
             nc.vector.tensor_scalar_max(v, v, 0.0)
 
         def quant_h(m, h, j0, j1):
+            if m not in hc:
+                hc[m] = wt_("hc", [P, G, W], U32)
+                hsc[m] = wt_("hsc", [P, G, W], U8)
             cols = slice(j0 * P, j1 * P)
             nc.vector.quantize_mx(
                 out=hc[m][:, h, cols].bitcast(FP8X4), scales=hsc[m][:, h, cols],
                 in_=hp[m, h][:, j0:j1].rearrange("p j r t -> p (j r t)"),
             )
 
-        st, sz, zt, pr = {}, {}, {}, {}
-
         def tint(m, c):
-            if c == 0:
-                st[m] = wt_("st", [P, NC, W], F32)
-            acc = bank("zt", 4)
+            bk["TN", m, c] = bank("zt", 4)
             for g in range(G):
                 nc.tensor.matmul_mx(
-                    out=acc[:],
+                    out=bk["TN", m, c][:],
                     lhsT=wt[:, g, 2 * c * P : 2 * (c + 1) * P].bitcast(FP4X4),
                     lhsT_scale=wts[:, g, c * P : (c + 1) * P],
                     rhs=xc[m][:, g].bitcast(FP8X4),
@@ -208,18 +304,19 @@ def tile_nerf_view_colour_head_f7_kernel(
                     start=(g == 0),
                     stop=(g == G - 1),
                 )
-            nc.scalar.activation(out=st[m][:, c], in_=acc[:], func=ACT.Sigmoid, bias=bcol[:, c : c + 1])
+
+        def shade(m, c):
+            if m not in st:
+                st[m] = wt_("st", [P, NC, W], F32, bufs=3)
+            nc.scalar.activation(out=st[m][:, c], in_=bk["TN", m, c][:], func=ACT.Sigmoid, bias=bcol[:, c : c + 1])
 
         def radiance(m, c, j0, j1):
-            if c == 0 and j0 == 0:
-                sz[m] = wt_("sz", [P, NC, W], F32)
             if j0 == 0:
-                zt[m, c] = bank("zt", 4)
-            acc = zt[m, c]
+                bk["Z", m, c] = bank("zt", 4)
             cols = slice(j0 * P, j1 * P)
             for h in range(G):
                 nc.tensor.matmul_mx(
-                    out=acc[:, cols],
+                    out=bk["Z", m, c][:, cols],
                     lhsT=wo[:, h, 4 * c * P : 4 * (c + 1) * P].bitcast(FP8X4),
                     lhsT_scale=wos[:, h, c * P : (c + 1) * P],
                     rhs=hc[m][:, h, cols].bitcast(FP8X4),
@@ -227,242 +324,129 @@ def tile_nerf_view_colour_head_f7_kernel(
                     start=(h == 0),
                     stop=(h == G - 1),
                 )
+
+        def sigmoid(m, c, j0, j1):
+            if m not in sz:
+                sz[m] = wt_("sz", [P, NC, W], F32, bufs=3)
+            cols = slice(j0 * P, j1 * P)
             nc.scalar.activation(
-                out=sz[m][:, c, cols], in_=acc[:, cols], func=ACT.Sigmoid, bias=bcol[:, NC + c : NC + c + 1]
+                out=sz[m][:, c, cols], in_=bk["Z", m, c][:, cols], func=ACT.Sigmoid, bias=bcol[:, NC + c : NC + c + 1]
             )
 
-        def log(m, c, j0=0, j1=NJ):
+        def log(m, c, j0, j1):
             v = sz[m][:, c, j0 * P : j1 * P]
             nc.scalar.activation(out=v, in_=v, func=ACT.Ln, bias=TINY)
 
-        def softplus(m, c, j0=0, j1=NJ):
-            if c == 0 and j0 == 0:
-                pr[m] = wt_("pr", [P, NC, W], F32)
+        def softplus(m, c, j0, j1):
+            if m not in pr:
+                pr[m] = wt_("pr", [P, NC, W], F32, bufs=3)
             cols = slice(j0 * P, j1 * P)
             nc.vector.scalar_tensor_tensor(
-                out=pr[m][:, c, cols], in0=zt[m, c][:, cols], scalar=bcol[:, NC + c : NC + c + 1],
+                out=pr[m][:, c, cols], in0=bk["Z", m, c][:, cols], scalar=bcol[:, NC + c : NC + c + 1],
                 in1=sz[m][:, c, cols], op0=ALU.add, op1=ALU.subtract,
             )
 
-        def product(eng, m, c, j0=0, j1=NJ):
+        def product(m, c, j0, j1):
             v = pr[m][:, c, j0 * P : j1 * P]
+            eng = nc.vector if m == NM - 1 else nc.gpsimd
             eng.tensor_tensor(out=v, in0=v, in1=st[m][:, c, j0 * P : j1 * P], op=ALU.mult)
 
-        def emit(m, j, on_vector=False):
-            tp = bank("tp", 2)
+        def turn_out(m, j):
+            bk["O", m, j] = bank("tp", 2)
             for c in range(NC):
-                nc.tensor.transpose(tp[:, c * P : (c + 1) * P], pr[m][:, c, j * P : (j + 1) * P], ident[:])
-            ot = wt_("ot", [P, C], F32, bufs=4)
-            if on_vector:
-                nc.vector.tensor_scalar_max(ot[:], tp[:], 0.0)
+                nc.tensor.transpose(bk["O", m, j][:, c * P : (c + 1) * P], pr[m][:, c, j * P : (j + 1) * P], ident[:])
+
+        def store(m, j):
+            ot = wt_("ot", [P, C], F32, bufs=8)
+            if (m, j) in ON_VECTOR:
+                nc.vector.tensor_scalar_max(ot[:], bk["O", m, j][:], 0.0)
             else:
-                nc.scalar.activation(out=ot[:], in_=tp[:], func=ACT.Relu)
+                nc.scalar.activation(out=ot[:], in_=bk["O", m, j][:], func=ACT.Relu)
             nc.sync.dma_start(out=ov[:, NJ * m + j, :], in_=ot[:])
 
-        em = kt("em", [P, E], F32)
-        eb = kt("eb", [P, E], BF16)
-        eg = kt("eg", [P, P, 4], BF16)
-        ec = kt("ec", [P, P], U32)
-        esc = kt("esc", [P, P], U8)
-        vw = kt("vw", [P, G, 4, P], F32)
-        hE = E // 2
+        pieces = {}
 
-        nc.scalar.activation(out=em[:, 0:hE], in_=ph[:], func=ACT.Sin)
-        nc.scalar.activation(out=em[:, hE:E], in_=ph[:], func=ACT.Abs)
-        nc.scalar.activation(out=em[:, hE:E], in_=em[:, hE:E], func=ACT.Sin, bias=math.pi / 2, scale=-1.0)
+        def piece(name, run, needs=(), takes=None, frees=None):
+            pieces[name] = (run, needs, takes)
+            if frees:
+                freed_by[frees] = name
 
-        def permute_scales(g):
-            nc.vector.tensor_copy(
-                out=wbsp[:, g].rearrange("p (h t m) -> p h t m", h=G, t=4),
-                in_=wbs[:, g].rearrange("p (h m t) -> p h t m", h=G, t=4),
-            )
-
-        def permute(g, h):
-            nc.vector.tensor_copy(
-                out=wbp[:, g, 1024 * h : 1024 * (h + 1)].rearrange("p (t m b) -> p t m b", t=4, b=2),
-                in_=wb[:, g, 1024 * h : 1024 * (h + 1)].rearrange("p (m t b) -> p t m b", t=4, b=2),
-            )
-
-        def view_product(h):
-            acc = bank("acc", 2)
-            nc.tensor.matmul_mx(
-                out=acc[:], lhsT=ec[:].bitcast(FP8X4), lhsT_scale=esc[:],
-                rhs=wv[:, 1024 * h : 1024 * (h + 1)].bitcast(FP4X4), rhs_scale=wvs[:, 512 * h : 512 * (h + 1)],
-                start=True, stop=True,
-            )
-            return acc
-
-        def view_out(h, acc):
-            nc.scalar.copy(out=vw[:, h], in_=acc[:].rearrange("p (m t) -> p t m", t=4))
-
-        def view_turn(h):
-            tp = bank("tp", 2)
-            for t in range(4):
-                nc.tensor.transpose(tp[:, t * P : (t + 1) * P], vw[:, h, t], ident[:])
-            return tp
-
-        def view_bias(h, tp):
-            nc.vector.tensor_tensor(
-                out=vb[:, h], in0=tp[:].rearrange("p (t r) -> p r t", t=4),
-                in1=hb[:, h].unsqueeze(1).to_broadcast([P, P, 4]), op=ALU.add,
-            )
-
-        xbs, tps, accs = {}, {}, {}
-
-        def wide(m, j):
-            if m < NM:
-                xbs[m, j] = widen(m, j)
-
-        def tr(m, j):
-            if m < NM:
-                tps[m, j] = turn(m, j, xbs[m, j])
-
-        def wr(m, j):
-            if m < NM:
-                words(m, j, tps[m, j])
-
-        def qx(m, g):
-            if m < NM:
-                quant_x(m, g)
-
-        def mul(m, h, j):
-            if m < NM:
-                accs[m, h, j] = bottleneck(m, h, j)
-
-        def add(m, h, j):
-            add_view(m, h, j, accs[m, h, j])
-
-        def tn(m, c):
-            if m < NM:
-                tint(m, c)
-
-        def soft(m, c):
-            if m >= 0:
-                log(m, c)
-                softplus(m, c)
-
-        def prod(m, c):
-            if m >= 0:
-                product(nc.gpsimd, m, c)
-
-        def em_(m, j):
-            if m >= 0:
-                emit(m, j)
-
-        def finish(m, j0, j1):
-            relu(m, 0, j0, j1)
-            relu(m, 1, j0, j1)
-            quant_h(m, 0, j0, j1)
-            quant_h(m, 1, j0, j1)
-            for c in range(NC):
-                radiance(m, c, j0, j1)
-
-        wide(0, 0)
-        tr(0, 0)
-        nc.vector.tensor_tensor(out=eb[:], in0=em[:], in1=gain[:], op=ALU.mult)
-        tp = bank("tp", 2)
-        ew = eb[:].bitcast(F32)
-        for u in range(2):
-            nc.tensor.transpose(tp[:, u * P : (u + 1) * P], ew[:, u:256:2], ident[:])
-        nc.scalar.copy(
-            out=eg[:].rearrange("p r t -> p (r t)").bitcast(F32).rearrange("p (r u) -> p r u", u=2),
-            in_=tp[:, 0:256].rearrange("p (u r) -> p r u", u=2),
-        )
-        wide(0, 1)
-        wr(0, 0)
-        tr(0, 1)
-        wide(0, 2)
-        tr(0, 2)
-        wide(0, 3)
-        wr(0, 1)
-        tr(0, 3)
-        permute_scales(0)
-        nc.vector.quantize_mx(out=ec[:].bitcast(FP8X4), scales=esc[:], in_=eg[:].rearrange("p r t -> p (r t)"))
-        permute(0, 0)
-        va0 = view_product(0)
-        permute(1, 0)
-        va1 = view_product(1)
-        wr(0, 2)
-        wr(0, 3)
-        qx(0, 0)
-        view_out(0, va0)
-        vt0 = view_turn(0)
-        view_out(1, va1)
-        vt1 = view_turn(1)
-        qx(0, 1)
-        view_bias(0, vt0)
-        bp = psum.tile([P, P], BF16, name="bp", tag="tp", bufs=2)
-        nc.tensor.transpose(bp[:], brow[:], identb[:])
-        nc.scalar.copy(out=bcol[:], in_=bp[:, 0 : 2 * NC])
-        tn(0, 0)
-        tn(0, 1)
-        permute_scales(1)
-        mul(0, 0, 0)
-        tn(0, 2)
-        permute(0, 1)
-        permute(1, 1)
-        mul(0, 1, 0)
-        view_bias(1, vt1)
-
+        freed_by = {}
+        piece(("XT", 0, 0), turn_scales, takes="tp")
+        piece(("XC", 0, 0), scale_columns, [("XT", 0, 0)], frees=("XT", 0, 0))
+        for v in range(2):
+            piece(("XU", 0, v), lambda v=v: spread_scales(v), [("XC", 0, 0)], takes="tp")
+            piece(("XW", 0, v), lambda v=v: scales_out(v), [("XU", 0, v)], frees=("XU", 0, v))
+        piece(("SIN", 0, 0), sines)
+        piece(("ET", 0, 0), turn_embed, [("SIN", 0, 0)], takes="tp")
+        piece(("EB", 0, 0), embed, [("ET", 0, 0)], frees=("ET", 0, 0))
+        piece(("EQ", 0, 0), quant_embed, [("EB", 0, 0)])
+        for h in range(G):
+            piece(("VM", 0, h), lambda h=h: view_product(h), [("EQ", 0, 0)], takes="acc")
+            piece(("VC", 0, h), lambda h=h: view_out(h), [("VM", 0, h)], frees=("VM", 0, h))
+            piece(("VT", 0, h), lambda h=h: view_turn(h), [("VC", 0, h)], takes="tp")
+            piece(("VB", 0, h), lambda h=h: view_done(h), [("VT", 0, h)], frees=("VT", 0, h))
+            piece(("PS", 0, h), lambda h=h: permute_scales(h))
+        for i in range(2 * G):
+            piece(("PW", 0, i), lambda i=i: permute(i))
+        piece(("BT", 0, 0), turn_bias, takes="tp")
+        piece(("BC", 0, 0), bias_columns, [("BT", 0, 0)], frees=("BT", 0, 0))
         for m in range(NM):
-            n, p, q = m + 1, m - 1, m - 2
-            wide(n, 0)
-            tr(n, 0)
-            wide(n, 1)
-            tr(n, 1)
-            add(m, 0, 0)
-            mul(m, 0, 1)
-            add(m, 1, 0)
-            mul(m, 0, 2)
-            wide(n, 2)
-            wr(n, 0)
-            tr(n, 2)
-            add(m, 0, 1)
-            mul(m, 1, 1)
-            wide(n, 3)
-            wr(n, 1)
-            tr(n, 3)
-            add(m, 0, 2)
-            mul(m, 0, 3)
-            add(m, 1, 1)
-            mul(m, 1, 2)
-            soft(p, 0)
-            soft(p, 1)
-            wr(n, 2)
-            wr(n, 3)
-            qx(n, 0)
-            prod(p, 0)
-            soft(p, 2)
-            soft(p, 3)
-            em_(q, 0)
-            prod(p, 1)
-            em_(q, 1)
-            tn(m, 3)
-            prod(p, 2)
-            prod(p, 3)
-            add(m, 0, 3)
-            mul(m, 1, 3)
-            qx(n, 1)
-            tn(n, 0)
-            tn(n, 1)
-            if n == NM:
-                finish(m, 0, 2)
-            add(m, 1, 2)
-            mul(n, 0, 0)
-            tn(n, 2)
-            add(m, 1, 3)
-            mul(n, 1, 0)
-            em_(q, 2)
-            em_(q, 3)
-            finish(m, 0 if n < NM else 2, NJ)
-        m = NM - 1
-        for j in range(NJ):
-            emit(m - 1, j, on_vector=True)
-        for j in (0, 2):
+            for j in range(NJ):
+                piece(("W", m, j), lambda m=m, j=j: widen(m, j), [("XW", 0, 0), ("XW", 0, 1)])
+                piece(("T", m, j), lambda m=m, j=j: turn(m, j), [("W", m, j)], takes="tp")
+                piece(("C", m, j), lambda m=m, j=j: words(m, j), [("T", m, j)], frees=("T", m, j))
+            for g in range(G):
+                piece(("QX", m, g), lambda m=m, g=g: quant_x(m, g), [("C", m, j) for j in range(NJ)])
+            both_x = [("QX", m, g) for g in range(G)]
+            parts = PARTS if m == NM - 1 else [(0, NJ)]
+            for h in range(G):
+                weights = [("PS", 0, 0), ("PS", 0, 1), ("PW", 0, 2 * h), ("PW", 0, 2 * h + 1)]
+                for j in range(NJ):
+                    piece((f"B{h}", m, j), lambda m=m, h=h, j=j: bottleneck(m, h, j), both_x + weights, takes="acc")
+                    piece((f"A{h}", m, j), lambda m=m, h=h, j=j: add_view(m, h, j), [(f"B{h}", m, j), ("VB", 0, h)], frees=(f"B{h}", m, j))
+                for v, (j0, j1) in enumerate(parts):
+                    piece((f"R{h}", m, v), lambda m=m, h=h, j0=j0, j1=j1: relu(m, h, j0, j1), [(f"A{h}", m, j) for j in range(j0, j1)])
+                    piece((f"QH{h}", m, v), lambda m=m, h=h, j0=j0, j1=j1: quant_h(m, h, j0, j1), [(f"R{h}", m, v)])
             for c in range(NC):
-                log(m, c, j, j + 2)
-                softplus(m, c, j, j + 2)
-            for c in range(NC):
-                product(nc.vector, m, c, j, j + 2)
-            emit(m, j)
-            emit(m, j + 1, on_vector=True)
+                piece(("TN", m, c), lambda m=m, c=c: tint(m, c), both_x, takes="zt")
+                piece(("SA", m, c), lambda m=m, c=c: shade(m, c), [("TN", m, c), ("BC", 0, 0)], frees=("TN", m, c))
+                for v, (j0, j1) in enumerate(parts):
+                    i = c + NC * v
+                    args = (m, c, j0, j1)
+                    piece(("Z", m, i), lambda a=args: radiance(*a), [("QH0", m, v), ("QH1", m, v)] + ([("Z", m, c)] if v else []), takes=None if v else "zt")
+                    piece(("SZ", m, i), lambda a=args: sigmoid(*a), [("Z", m, i)])
+                    piece(("L", m, i), lambda a=args: log(*a), [("SZ", m, i)])
+                    piece(("D", m, i), lambda a=args: softplus(*a), [("L", m, i)], frees=("Z", m, c) if j1 == NJ else None)
+                    piece(("P", m, i), lambda a=args: product(*a), [("D", m, i), ("SA", m, c)])
+            for j in range(NJ):
+                v = [j0 <= j < j1 for j0, j1 in parts].index(True)
+                piece(("O", m, j), lambda m=m, j=j: turn_out(m, j), [("P", m, c + NC * v) for c in range(NC)], takes="tp")
+                piece(("E", m, j), lambda m=m, j=j: store(m, j), [("O", m, j)], frees=("O", m, j))
+
+        banks = {"tp": 2, "acc": 2, "zt": 4}
+        tenants = {tag: [] for tag in banks}
+        issued = set()
+
+        def issue(name):
+            if name in issued:
+                return
+            issued.add(name)
+            run, needs, takes = pieces[name]
+            for other in needs:
+                issue(other)
+            if takes:
+                while len(tenants[takes]) >= banks[takes] and freed_by[tenants[takes][-banks[takes]]] not in issued:
+                    issue(freed_by[tenants[takes][-banks[takes]]])
+                tenants[takes].append(name)
+            run()
+
+        done = {}
+        for rnd in range(-2, NM + 2):
+            for token in ORDER.split():
+                stage = token.replace("+", "").replace("-", "")
+                m = rnd + (len(token) - len(stage)) * (1 if "+" in token else -1)
+                i = done.get((stage, m), 0)
+                done[stage, m] = i + 1
+                if (stage, m, i) in pieces:
+                    issue((stage, m, i))

import math
from contextlib import ExitStack

import concourse.mybir as mybir
from concourse.masks import make_identity

R, S, K, E, F, C = 128, 16, 1024, 512, 1024, 512
FLOPS = 2 * (R * E * F + R * S * K * (F + C) + R * S * F * C)

F32 = mybir.dt.float32
BF16 = mybir.dt.bfloat16
I32 = mybir.dt.int32
U32 = mybir.dt.uint32
U8 = mybir.dt.uint8
FP8 = mybir.dt.float8_e4m3fn
FP8X4 = mybir.dt.float8_e4m3fn_x4
FP4X4 = mybir.dt.float4_e2m1fn_x4
ALU = mybir.AluOpType
ACT = mybir.ActivationFunctionType

P = 128
G = 2
NJ = 4
NM = S // NJ
W = NJ * P
NC = C // P
TINY = 2.0**-64
PARTS = [(0, 2), (2, 4)]
ON_VECTOR = {(3, 1), (3, 3), (2, 0), (2, 1)}
ORDER = """
L- O-- O-- VM+ VT+ R0- L- SA E-- VT+ E-- SA D- XU+ E-- E-- B0+ SA+ B0+ SA+ R1 SIN+ SZ A1- Z-- Z D- QH1- A1--
SZ SZ W++ EB++ SZ VC W TN- T++ T++ C+ B0+ C TN+ T++ PW+ VC-- SZ QX B0+ B1+ XW-- Z- XW- L- P-- SZ QH0 T++ SZ SZ
BC++ Z- QH1- R1 BT-- B1+ VB+ VM++ P-- L D- PS++ C++ TN+ PW++ D- B1+ P-- R0+ P-- O- A0-- XU+ ET++ P- QH0 Z- L
L-- A0-- O- XC+ D- TN+ PS++ XT-- W Z- PW+ A1 W-- C+ A1+ L-- D- P- EQ+ PW++ B1+ A0-- P- Z D- QX++ A0+ VB D- P-
Z L
"""


def tile_nerf_view_colour_head_f7_kernel(
    tc, x_bytes, x_scale, phase, band_gain, wb_words, wb_scales, wv_words, wv_scales, hidden_bias,
    wt_words, wt_scales, tint_bias, wo_words, wo_scales, colour_bias, out,
):
    nc = tc.nc
    with ExitStack() as ctx:
        keep = ctx.enter_context(tc.tile_pool(name="keep", bufs=1))
        work = ctx.enter_context(tc.tile_pool(name="work", bufs=2))
        psum = ctx.enter_context(tc.psum_pool(name="psum", bufs=2))
        ctx.enter_context(tc.manual_schedule())

        def kt(name, shape, dtype):
            return keep.tile(shape, dtype, name=name, align_bytes=64)

        def wt_(name, shape, dtype, bufs=2):
            return work.tile(shape, dtype, name=name, align_bytes=64, bufs=bufs)

        def bank(tag, bufs):
            return psum.tile([P, 512], F32, name=tag, bufs=bufs)

        ident = kt("ident", [P, P], F32)
        identb = kt("identb", [P, P], BF16)
        xs = kt("xs", [P, K], F32)
        xraw = [kt(f"xraw{m}", [P, NJ * K], U8) for m in range(NM)]
        ph = kt("ph", [P, E // 2], BF16)
        gain = kt("gain", [P, 4], BF16)
        hb = kt("hb", [P, G, 4], BF16)
        srow = kt("srow", [P, P], F32)
        scol = kt("scol", [P, K // P], F32)
        brow = kt("brow", [P, P], BF16)
        bcol = kt("bcol", [P, 2 * NC], F32)
        wb = kt("wb", [P, G, 2 * F], U8)
        wbs = kt("wbs", [P, G, F], U8)
        wbp = kt("wbp", [P, G, 2 * F], U8)
        wbsp = kt("wbsp", [P, G, F], U8)
        wv = kt("wv", [P, 2 * F], U8)
        wvs = kt("wvs", [P, F], U8)
        wt = kt("wt", [P, G, 2 * C], U8)
        wts = kt("wts", [P, G, C], U8)
        wo = kt("wo", [P, G, 4 * C], U8)
        wos = kt("wos", [P, G, C], U8)
        vb = kt("vb", [P, G, P, 4], F32)

        xv = x_bytes.rearrange("(r s) k -> r (s k)", s=S)
        ov = out.rearrange("(r s) c -> r s c", s=S)

        def load_scales(tile_, dram):
            for q in range(4):
                nc.sync.dma_start(
                    out=tile_[32 * q : 32 * q + 4].bitcast(I32),
                    in_=dram[:, 4 * q : 4 * q + 4, :].rearrange("g q n -> q g n").bitcast(I32),
                )

        def load_x(m, j0, j1):
            nc.sync.dma_start(out=xraw[m][:, j0 * K : j1 * K], in_=xv[:, (m * NJ + j0) * K : (m * NJ + j1) * K])

        warm = kt("warm", [P, 1], F32)
        nc.vector.memset(srow[:], 0.0)
        nc.vector.memset(warm[:], 0.0)
        nc.scalar.activation(out=warm[:], in_=warm[:], func=ACT.Sin)
        make_identity(nc, ident[:])
        nc.vector.memset(wbs[:].rearrange("p g n -> p (g n)").bitcast(I32), 0)
        nc.vector.memset(wvs[:].bitcast(I32), 0)
        nc.vector.memset(brow[:], 0.0)
        for t_ in (wts, wos):
            nc.vector.memset(t_[:].rearrange("p g n -> p (g n)").bitcast(I32), 0)
        nc.gpsimd.tensor_copy(out=identb[:], in_=ident[:])

        nc.sync.dma_start(out=srow[0 : K // P, :], in_=x_scale.rearrange("o (a p) -> (o a) p", p=P))
        nc.sync.dma_start(out=ph[:], in_=phase)
        load_x(0, 0, 2)
        load_x(0, 2, 4)
        nc.sync.dma_start(out=gain[:], in_=band_gain.rearrange("(p t) -> p t", t=4))
        nc.sync.dma_start(out=wb[:].bitcast(I32), in_=wb_words.rearrange("g p n -> p g n").bitcast(I32))
        nc.sync.dma_start(out=wv[:].bitcast(I32), in_=wv_words[0].bitcast(I32))
        load_scales(wbs, wb_scales)
        for q in range(4):
            nc.sync.dma_start(out=wvs[32 * q : 32 * q + 4].bitcast(I32), in_=wv_scales[0, 4 * q : 4 * q + 4, :].bitcast(I32))
        nc.sync.dma_start(out=hb[:], in_=hidden_bias.rearrange("(g p t) -> p g t", g=G, t=4))
        nc.sync.dma_start(out=brow[0:NC, :], in_=tint_bias.rearrange("(a p) -> a p", p=P))
        nc.sync.dma_start(out=brow[NC : 2 * NC, :], in_=colour_bias.rearrange("(a p) -> a p", p=P))
        load_scales(wts, wt_scales)
        nc.sync.dma_start(out=wt[:].bitcast(I32), in_=wt_words.rearrange("g p n -> p g n").bitcast(I32))
        load_x(1, 0, 4)
        load_scales(wos, wo_scales)
        nc.sync.dma_start(
            out=wo[:].bitcast(I32), in_=wo_words.rearrange("g p n t -> p g (n t)").bitcast(I32)
        )
        for m in range(2, NM):
            load_x(m, 0, 4)

        em = kt("em", [P, 4, P], F32)
        eg = kt("eg", [P, P, 4], BF16)
        ec = kt("ec", [P, P], U32)
        esc = kt("esc", [P, P], U8)
        vw = kt("vw", [P, G, 4, P], F32)
        half = P // 2
        bk = {}
        xb, xg, xc, xsc, hp, hc, hsc, st, sz, pr = {}, {}, {}, {}, {}, {}, {}, {}, {}, {}

        def turn_scales():
            bk["XT"] = bank("tp", 2)
            nc.tensor.transpose(bk["XT"][:, 0:P], srow[:], ident[:])

        def scale_columns():
            nc.scalar.copy(out=scol[:], in_=bk["XT"][:, 0 : K // P])

        def spread_scales(v):
            bk["XU", v] = bank("tp", 2)
            for a in range(4):
                nc.tensor.transpose(
                    bk["XU", v][:, a * P : (a + 1) * P], scol[:, 4 * v + a : 4 * v + a + 1].to_broadcast([P, P]), ident[:]
                )

        def scales_out(v):
            cols = slice(512 * v, 512 * (v + 1))
            if v == 0:
                nc.scalar.copy(out=xs[:, cols], in_=bk["XU", v][:])
            else:
                nc.vector.tensor_copy(out=xs[:, cols], in_=bk["XU", v][:])

        def sines():
            angle = ph[:].rearrange("r (p t) -> r t p", t=4)
            nc.scalar.activation(out=em[:, :, 0:half], in_=angle, func=ACT.Sin)
            nc.scalar.activation(out=em[:, :, half:P], in_=angle, func=ACT.Abs)
            nc.scalar.activation(
                out=em[:, :, half:P], in_=em[:, :, half:P], func=ACT.Sin, bias=math.pi / 2, scale=-1.0
            )

        def turn_embed():
            bk["E"] = bank("tp", 2)
            for t in range(4):
                nc.tensor.transpose(bk["E"][:, t * P : (t + 1) * P], em[:, t], ident[:])

        def embed():
            nc.vector.tensor_tensor(
                out=eg[:], in0=bk["E"][:].rearrange("p (t r) -> p r t", t=4),
                in1=gain[:].unsqueeze(1).to_broadcast([P, P, 4]), op=ALU.mult,
            )

        def quant_embed():
            nc.vector.quantize_mx(out=ec[:].bitcast(FP8X4), scales=esc[:], in_=eg[:].rearrange("p r t -> p (r t)"))

        def view_product(h):
            bk["VM", h] = bank("acc", 2)
            nc.tensor.matmul_mx(
                out=bk["VM", h][:], lhsT=ec[:].bitcast(FP8X4), lhsT_scale=esc[:],
                rhs=wv[:, 1024 * h : 1024 * (h + 1)].bitcast(FP4X4), rhs_scale=wvs[:, 512 * h : 512 * (h + 1)],
                start=True, stop=True,
            )

        def view_out(h):
            nc.scalar.copy(out=vw[:, h], in_=bk["VM", h][:].rearrange("p (m t) -> p t m", t=4))

        def view_turn(h):
            bk["VT", h] = bank("tp", 2)
            for t in range(4):
                nc.tensor.transpose(bk["VT", h][:, t * P : (t + 1) * P], vw[:, h, t], ident[:])

        def view_done(h):
            nc.vector.tensor_tensor(
                out=vb[:, h], in0=bk["VT", h][:].rearrange("p (t r) -> p r t", t=4),
                in1=hb[:, h].unsqueeze(1).to_broadcast([P, P, 4]), op=ALU.add,
            )

        def permute_scales(g):
            nc.vector.tensor_copy(
                out=wbsp[:, g].rearrange("p (h t m) -> p h t m", h=G, t=4),
                in_=wbs[:, g].rearrange("p (h m t) -> p h t m", h=G, t=4),
            )

        def permute(i):
            h, g = divmod(i, G)
            cols = slice(1024 * h, 1024 * (h + 1))
            nc.vector.tensor_copy(
                out=wbp[:, g, cols].rearrange("p (t m b) -> p t m b", t=4, b=2),
                in_=wb[:, g, cols].rearrange("p (m t b) -> p t m b", t=4, b=2),
            )

        def turn_bias():
            bk["BT"] = psum.tile([P, P], BF16, name="bp", tag="tp", bufs=2)
            nc.tensor.transpose(bk["BT"][:], brow[:], identb[:])

        def bias_columns():
            nc.scalar.copy(out=bcol[:], in_=bk["BT"][:, 0 : 2 * NC])

        def widen(m, j):
            xb[m, j] = wt_("xb", [P, K], BF16, bufs=6)
            nc.vector.tensor_tensor(
                out=xb[m, j][:], in0=xraw[m][:, j * K : (j + 1) * K].bitcast(FP8), in1=xs[:], op=ALU.mult
            )

        def turn(m, j):
            xw = xb[m, j][:].bitcast(F32)
            bk["T", m, j] = bank("tp", 2)
            for g in range(G):
                for u in range(2):
                    nc.tensor.transpose(
                        bk["T", m, j][:, (2 * g + u) * P : (2 * g + u + 1) * P],
                        xw[:, 256 * g + u : 256 * (g + 1) : 2], ident[:],
                    )

        def words(m, j):
            if m not in xg:
                xg[m] = wt_("xg", [P, G, NJ, P, 4], BF16, bufs=3)
            nc.scalar.copy(
                out=xg[m][:, :, j].rearrange("p g r t -> p g (r t)").bitcast(F32).rearrange("p g (r u) -> p g r u", u=2),
                in_=bk["T", m, j][:].rearrange("p (g u r) -> p g r u", g=G, u=2),
            )

        def quant_x(m, g):
            if m not in xc:
                xc[m] = wt_("xc", [P, G, W], U32, bufs=3)
                xsc[m] = wt_("xsc", [P, G, W], U8, bufs=3)
            nc.vector.quantize_mx(
                out=xc[m][:, g].bitcast(FP8X4), scales=xsc[m][:, g],
                in_=xg[m][:, g].rearrange("p j r t -> p (j r t)"),
            )

        def bottleneck(m, h, j):
            acc = bk["B", m, h, j] = bank("acc", 2)
            cols = slice(j * P, (j + 1) * P)
            for t in range(4):
                n0 = (h * 4 + t) * P
                for g in range(G):
                    nc.tensor.matmul_mx(
                        out=acc[:, t * P : (t + 1) * P],
                        lhsT=wbp[:, g, 2 * n0 : 2 * (n0 + P)].bitcast(FP4X4),
                        lhsT_scale=wbsp[:, g, n0 : n0 + P],
                        rhs=xc[m][:, g, cols].bitcast(FP8X4),
                        rhs_scale=xsc[m][:, g, cols],
                        start=(g == 0),
                        stop=(g == G - 1),
                    )

        def add_view(m, h, j):
            if (m, h) not in hp:
                hp[m, h] = wt_("hp", [P, NJ, P, 4], BF16, bufs=4)
            nc.vector.tensor_tensor(
                out=hp[m, h][:, j], in0=bk["B", m, h, j][:].rearrange("p (t r) -> p r t", t=4), in1=vb[:, h], op=ALU.add
            )

        def relu(m, h, j0, j1):
            v = hp[m, h][:, j0:j1].rearrange("p j r t -> p (j r t)")
            nc.vector.tensor_scalar_max(v, v, 0.0)

        def quant_h(m, h, j0, j1):
            if m not in hc:
                hc[m] = wt_("hc", [P, G, W], U32)
                hsc[m] = wt_("hsc", [P, G, W], U8)
            cols = slice(j0 * P, j1 * P)
            nc.vector.quantize_mx(
                out=hc[m][:, h, cols].bitcast(FP8X4), scales=hsc[m][:, h, cols],
                in_=hp[m, h][:, j0:j1].rearrange("p j r t -> p (j r t)"),
            )

        def tint(m, c):
            bk["TN", m, c] = bank("zt", 4)
            for g in range(G):
                nc.tensor.matmul_mx(
                    out=bk["TN", m, c][:],
                    lhsT=wt[:, g, 2 * c * P : 2 * (c + 1) * P].bitcast(FP4X4),
                    lhsT_scale=wts[:, g, c * P : (c + 1) * P],
                    rhs=xc[m][:, g].bitcast(FP8X4),
                    rhs_scale=xsc[m][:, g],
                    start=(g == 0),
                    stop=(g == G - 1),
                )

        def shade(m, c):
            if m not in st:
                st[m] = wt_("st", [P, NC, W], F32, bufs=3)
            nc.scalar.activation(out=st[m][:, c], in_=bk["TN", m, c][:], func=ACT.Sigmoid, bias=bcol[:, c : c + 1])

        def radiance(m, c, j0, j1):
            if j0 == 0:
                bk["Z", m, c] = bank("zt", 4)
            cols = slice(j0 * P, j1 * P)
            for h in range(G):
                nc.tensor.matmul_mx(
                    out=bk["Z", m, c][:, cols],
                    lhsT=wo[:, h, 4 * c * P : 4 * (c + 1) * P].bitcast(FP8X4),
                    lhsT_scale=wos[:, h, c * P : (c + 1) * P],
                    rhs=hc[m][:, h, cols].bitcast(FP8X4),
                    rhs_scale=hsc[m][:, h, cols],
                    start=(h == 0),
                    stop=(h == G - 1),
                )

        def sigmoid(m, c, j0, j1):
            if m not in sz:
                sz[m] = wt_("sz", [P, NC, W], F32, bufs=3)
            cols = slice(j0 * P, j1 * P)
            nc.scalar.activation(
                out=sz[m][:, c, cols], in_=bk["Z", m, c][:, cols], func=ACT.Sigmoid, bias=bcol[:, NC + c : NC + c + 1]
            )

        def log(m, c, j0, j1):
            v = sz[m][:, c, j0 * P : j1 * P]
            nc.scalar.activation(out=v, in_=v, func=ACT.Ln, bias=TINY)

        def softplus(m, c, j0, j1):
            if m not in pr:
                pr[m] = wt_("pr", [P, NC, W], F32, bufs=3)
            cols = slice(j0 * P, j1 * P)
            nc.vector.scalar_tensor_tensor(
                out=pr[m][:, c, cols], in0=bk["Z", m, c][:, cols], scalar=bcol[:, NC + c : NC + c + 1],
                in1=sz[m][:, c, cols], op0=ALU.add, op1=ALU.subtract,
            )

        def product(m, c, j0, j1):
            v = pr[m][:, c, j0 * P : j1 * P]
            eng = nc.vector if m == NM - 1 else nc.gpsimd
            eng.tensor_tensor(out=v, in0=v, in1=st[m][:, c, j0 * P : j1 * P], op=ALU.mult)

        def turn_out(m, j):
            bk["O", m, j] = bank("tp", 2)
            for c in range(NC):
                nc.tensor.transpose(bk["O", m, j][:, c * P : (c + 1) * P], pr[m][:, c, j * P : (j + 1) * P], ident[:])

        def store(m, j):
            ot = wt_("ot", [P, C], F32, bufs=8)
            if (m, j) in ON_VECTOR:
                nc.vector.tensor_scalar_max(ot[:], bk["O", m, j][:], 0.0)
            else:
                nc.scalar.activation(out=ot[:], in_=bk["O", m, j][:], func=ACT.Relu)
            nc.sync.dma_start(out=ov[:, NJ * m + j, :], in_=ot[:])

        pieces = {}

        def piece(name, run, needs=(), takes=None, frees=None):
            pieces[name] = (run, needs, takes)
            if frees:
                freed_by[frees] = name

        freed_by = {}
        piece(("XT", 0, 0), turn_scales, takes="tp")
        piece(("XC", 0, 0), scale_columns, [("XT", 0, 0)], frees=("XT", 0, 0))
        for v in range(2):
            piece(("XU", 0, v), lambda v=v: spread_scales(v), [("XC", 0, 0)], takes="tp")
            piece(("XW", 0, v), lambda v=v: scales_out(v), [("XU", 0, v)], frees=("XU", 0, v))
        piece(("SIN", 0, 0), sines)
        piece(("ET", 0, 0), turn_embed, [("SIN", 0, 0)], takes="tp")
        piece(("EB", 0, 0), embed, [("ET", 0, 0)], frees=("ET", 0, 0))
        piece(("EQ", 0, 0), quant_embed, [("EB", 0, 0)])
        for h in range(G):
            piece(("VM", 0, h), lambda h=h: view_product(h), [("EQ", 0, 0)], takes="acc")
            piece(("VC", 0, h), lambda h=h: view_out(h), [("VM", 0, h)], frees=("VM", 0, h))
            piece(("VT", 0, h), lambda h=h: view_turn(h), [("VC", 0, h)], takes="tp")
            piece(("VB", 0, h), lambda h=h: view_done(h), [("VT", 0, h)], frees=("VT", 0, h))
            piece(("PS", 0, h), lambda h=h: permute_scales(h))
        for i in range(2 * G):
            piece(("PW", 0, i), lambda i=i: permute(i))
        piece(("BT", 0, 0), turn_bias, takes="tp")
        piece(("BC", 0, 0), bias_columns, [("BT", 0, 0)], frees=("BT", 0, 0))
        for m in range(NM):
            for j in range(NJ):
                piece(("W", m, j), lambda m=m, j=j: widen(m, j), [("XW", 0, 0), ("XW", 0, 1)])
                piece(("T", m, j), lambda m=m, j=j: turn(m, j), [("W", m, j)], takes="tp")
                piece(("C", m, j), lambda m=m, j=j: words(m, j), [("T", m, j)], frees=("T", m, j))
            for g in range(G):
                piece(("QX", m, g), lambda m=m, g=g: quant_x(m, g), [("C", m, j) for j in range(NJ)])
            both_x = [("QX", m, g) for g in range(G)]
            parts = PARTS if m == NM - 1 else [(0, NJ)]
            for h in range(G):
                weights = [("PS", 0, 0), ("PS", 0, 1), ("PW", 0, 2 * h), ("PW", 0, 2 * h + 1)]
                for j in range(NJ):
                    piece((f"B{h}", m, j), lambda m=m, h=h, j=j: bottleneck(m, h, j), both_x + weights, takes="acc")
                    piece((f"A{h}", m, j), lambda m=m, h=h, j=j: add_view(m, h, j), [(f"B{h}", m, j), ("VB", 0, h)], frees=(f"B{h}", m, j))
                for v, (j0, j1) in enumerate(parts):
                    piece((f"R{h}", m, v), lambda m=m, h=h, j0=j0, j1=j1: relu(m, h, j0, j1), [(f"A{h}", m, j) for j in range(j0, j1)])
                    piece((f"QH{h}", m, v), lambda m=m, h=h, j0=j0, j1=j1: quant_h(m, h, j0, j1), [(f"R{h}", m, v)])
            for c in range(NC):
                piece(("TN", m, c), lambda m=m, c=c: tint(m, c), both_x, takes="zt")
                piece(("SA", m, c), lambda m=m, c=c: shade(m, c), [("TN", m, c), ("BC", 0, 0)], frees=("TN", m, c))
                for v, (j0, j1) in enumerate(parts):
                    i = c + NC * v
                    args = (m, c, j0, j1)
                    piece(("Z", m, i), lambda a=args: radiance(*a), [("QH0", m, v), ("QH1", m, v)] + ([("Z", m, c)] if v else []), takes=None if v else "zt")
                    piece(("SZ", m, i), lambda a=args: sigmoid(*a), [("Z", m, i)])
                    piece(("L", m, i), lambda a=args: log(*a), [("SZ", m, i)])
                    piece(("D", m, i), lambda a=args: softplus(*a), [("L", m, i)], frees=("Z", m, c) if j1 == NJ else None)
                    piece(("P", m, i), lambda a=args: product(*a), [("D", m, i), ("SA", m, c)])
            for j in range(NJ):
                v = [j0 <= j < j1 for j0, j1 in parts].index(True)
                piece(("O", m, j), lambda m=m, j=j: turn_out(m, j), [("P", m, c + NC * v) for c in range(NC)], takes="tp")
                piece(("E", m, j), lambda m=m, j=j: store(m, j), [("O", m, j)], frees=("O", m, j))

        banks = {"tp": 2, "acc": 2, "zt": 4}
        tenants = {tag: [] for tag in banks}
        issued = set()

        def issue(name):
            if name in issued:
                return
            issued.add(name)
            run, needs, takes = pieces[name]
            for other in needs:
                issue(other)
            if takes:
                while len(tenants[takes]) >= banks[takes] and freed_by[tenants[takes][-banks[takes]]] not in issued:
                    issue(freed_by[tenants[takes][-banks[takes]]])
                tenants[takes].append(name)
            run()

        done = {}
        for rnd in range(-2, NM + 2):
            for token in ORDER.split():
                stage = token.replace("+", "").replace("-", "")
                m = rnd + (len(token) - len(stage)) * (1 if "+" in token else -1)
                i = done.get((stage, m), 0)
                done[stage, m] = i + 1
                if (stage, m, i) in pieces:
                    issue((stage, m, i))
